import numpy as np
CORES = [4,5,6,7,0,1,2,3]
N = 8
def setup_inputs(rng):
    return {"x1": rng.standard_normal((N, 128, 64), dtype=np.float32), "x2": rng.standard_normal((N, 128, 2048), dtype=np.float32)}
def reference(x1, x2):
    out = []
    b = 64 // N
    bl = x1.reshape(N, 128, N, b)
    out.append(np.ascontiguousarray(bl.transpose(2, 1, 0, 3)).reshape(N, 128, 64))
    s = x2.sum(axis=0, dtype=np.float64).astype(x2.dtype)
    out.append(np.broadcast_to(s, (N,) + s.shape))
    return {"y1": out[0], "y2": out[1]}

from concourse.bass import DstId, RemoteDMATransfer
from concourse.mybir import AluOpType

N = 8
B1 = 8
B2 = 256
W = B2 + B1

SCRATCH = {
    "stage": ("sbuf", [128, N, W], "float32"),
    "land": ("sbuf", [128, N, W], "float32"),
    "res": ("sbuf", [128, N * B2], "float32"),
}
SEMAPHORES = ["loaded", "acc", "stored", "sent", "rs", "ag"]


def split_peers(r):
    peers = [j for j in range(N) if j != r]
    runs = [(a, s) for s in (1, 2, 3) for a in range(N) if all(a + k * s in peers for k in range(3))]
    for da, ds in runs:
        for sa, ss in runs:
            d = [da + k * ds for k in range(3)]
            s = [sa + k * ss for k in range(3)]
            if not set(d) & set(s):
                rest = [j for j in peers if j not in d and j not in s]
                return d, slice(da, da + 2 * ds + 1, ds), slice(sa, sa + 2 * ss + 1, ss), rest[0]
    raise ValueError("no split")


def rank_program(g, core, T, topo):
    r = T.rank_of(core)
    if r is None:
        return
    S = T.sem
    add = AluOpType.add
    peers = [j for j in range(N) if j != r]
    own2 = slice(r * B2, (r + 1) * B2)

    def dst(rank):
        rid, pid, sengine = topo.addr(T.cores[rank])
        return DstId(rid=rid, pnc=pid)

    g.dma_start(out=T.stage[:, :, 0:B2], in_=T.x2[:, :]).then_inc(S.loaded, 16)
    g.dma_start(out=T.stage[:, :, B2:W], in_=T.x1[:, :]).then_inc(S.loaded, 16)
    g.dma_start(out=T.land[:, r, B2:W], in_=T.x1[:, r * B1:(r + 1) * B1]).then_inc(S.loaded, 16)
    g.dma_start(out=T.y2[:, own2], in_=T.x2[:, own2]).then_inc(S.loaded, 16)
    g.wait_ge(S.loaded, 64)

    g.remote_dma_fused(
        [RemoteDMATransfer(dst_ids=[dst(j)], dma_engine_mask=3 << (2 * k), remote_sem=S.rs,
                           src=T.stage[:, j, :], dst=T.land[:, r, :])
         for k, j in enumerate(peers)],
        local_sem=S.sent)
    g.wait_ge(S.rs, 7 * 2)

    g.remote_dma_fused(
        [RemoteDMATransfer(dst_ids=[dst(j) for j in peers], dma_engine_mask=0xFFFF, remote_sem=S.ag,
                           srcs=[T.stage[:, r, 0:B2] if i == r else T.land[:, i, 0:B2] for i in range(N)],
                           dsts=[T.res[:, own2] for j in peers], alu_op=1)],
        local_sem=S.sent)

    g.dma_start(out=T.y1[:, :], in_=T.land[:, :, B2:W]).then_inc(S.stored, 16)

    d, dsl, ssl, rest = split_peers(r)
    g.dma_start(out=T.y2[:, own2], in_=T.land[:, rest, 0:B2], accum_op=add).then_inc(S.acc, 16)
    g.wait_ge(S.sent, 14 + 16)
    g.dma_start(out=T.land[:, dsl, 0:B2], in_=T.land[:, ssl, 0:B2], accum_op=add).then_inc(S.acc, 16)

    g.wait_ge(S.ag, 7 * 16)
    stores = 1
    if r > 0:
        g.dma_start(out=T.y2[:, 0:r * B2], in_=T.res[:, 0:r * B2]).then_inc(S.stored, 16)
        stores += 1
    if r < N - 1:
        g.dma_start(out=T.y2[:, (r + 1) * B2:], in_=T.res[:, (r + 1) * B2:]).then_inc(S.stored, 16)
        stores += 1

    g.wait_ge(S.acc, 32)
    g.dma_start(out=T.y2[:, own2], in_=T.land[:, d[2], 0:B2], accum_op=add).then_inc(S.acc, 16)
    g.dma_start(out=T.land[:, d[0], 0:B2], in_=T.land[:, d[1], 0:B2], accum_op=add).then_inc(S.acc, 16)
    g.wait_ge(S.acc, 64)
    g.dma_start(out=T.y2[:, own2], in_=T.land[:, d[0], 0:B2], accum_op=add).then_inc(S.acc, 16)
    g.wait_ge(S.acc, 80)
    g.wait_ge(S.stored, 16 * stores)
